import numpy as np
import ml_dtypes


def mxq(x, axis, fmt="e4m3"):
    dtype, down = {"e4m3": (ml_dtypes.float8_e4m3fn, 7), "e5m2": (ml_dtypes.float8_e5m2, 14)}[fmt]
    v = np.moveaxis(np.asarray(x, np.float32).astype(ml_dtypes.bfloat16).astype(np.float64), axis, -1)
    blocks = v.reshape(v.shape[:-1] + (-1, 32))
    amax = np.abs(blocks).max(-1, keepdims=True)
    byte = np.maximum(np.where(amax > 0, np.frexp(amax)[1] - 1 + 127, 0) - down, 1)
    scale = np.exp2(byte - 127.0)
    codes = (blocks / scale).astype(np.float32).astype(dtype).astype(np.float64)
    return np.moveaxis((codes * scale).reshape(v.shape), -1, axis)


WIDE = False


def mx_kscale(k):
    if not WIDE:
        return np.ones(k)
    levels = np.array([10, -10, 5, -5, 0])
    if k % 512:
        return np.exp2(np.random.permutation(np.resize(levels, k // 32))).repeat(32)
    a = np.empty((k // 512, 16))
    for p in range(k // 512):
        a[p, :8] = np.random.permutation(np.resize(levels, 8))
        for g in range(8):
            far = levels[np.abs(levels - a[p, g]) >= 10]
            a[p, g + 8] = far[np.random.randint(len(far))]
    return np.exp2(a.ravel()).repeat(32)


def f64(x):
    return np.asarray(x).astype(np.float64)


def striped(idx):
    return np.tile(idx.reshape(-1, 16).T, (8, 1)).astype(np.uint16)


def unstriped(offs):
    return offs[:16].T.reshape(-1).astype(np.int64)


E2M1 = np.array([0.0, 0.5, 1.0, 1.5, 2.0, 3.0, 4.0, 6.0, -0.0, -0.5, -1.0, -1.5, -2.0, -3.0, -4.0, -6.0])


def pack_weight(w, fmt):
    k, n = w.shape
    w = f64(np.asarray(w, np.float32).astype(ml_dtypes.bfloat16)).reshape(k // 32, 32, n)
    amax = np.abs(w).max(1)
    if fmt == "e4m3":
        byte = np.frexp(amax)[1] - 1 + 127 - 7
    else:
        mant, ex = np.frexp(amax / 6.0)
        byte = np.where(mant > 0.5, ex, ex - 1) + 127
    byte = np.clip(np.where(amax > 0, byte, 1), 1, 254)
    scaled = (w * np.exp2(127.0 - byte)[:, None, :]).reshape(k, n).astype(np.float32)
    by_word = np.ascontiguousarray(scaled.reshape(k // 512, 128, 4, n).transpose(0, 1, 3, 2))
    if fmt == "e4m3":
        words = by_word.astype(ml_dtypes.float8_e4m3fn).view(np.uint8)
    else:
        c = by_word.astype(ml_dtypes.float4_e2m1fn).view(np.uint8) & 0xF
        words = (c[..., 0::2] | (c[..., 1::2] << 4)).reshape(k // 512, 128, 2 * n)
    return np.ascontiguousarray(words), np.ascontiguousarray(byte.astype(np.uint8).reshape(k // 512, 16, n))


def unpack_weight(words, scales, fmt):
    g, _, n = scales.shape
    words = np.ascontiguousarray(words).reshape(g, 128, n, -1)
    if fmt == "e4m3":
        vals = words.view(ml_dtypes.float8_e4m3fn).astype(np.float64)
    else:
        nib = np.empty((g, 128, n, 4), np.uint8)
        nib[..., 0::2] = words & 0xF
        nib[..., 1::2] = words >> 4
        vals = E2M1[nib]
    vals = vals * np.repeat(np.exp2(scales.astype(np.float64) - 127.0), 8, axis=1)[..., None]
    return vals.transpose(0, 1, 3, 2).reshape(g * 512, n)


def gelu(v):
    return 0.5 * v * (1.0 + np.tanh(np.sqrt(2.0 / np.pi) * (v + 0.044715 * v**3)))


K, T, S, H, R, N = 1024, 4096, 1024, 512, 1024, 384

def setup_inputs():
    n = np.random.standard_normal
    s = mx_kscale(K)[:, None]
    u = mx_kscale(H)[:, None]
    u2 = mx_kscale(R)[:, None]
    d = {}
    d["tab_words"], d["tab_scales"] = pack_weight(n((K, T)) * s, "e4m3")
    d["offs"] = striped(np.random.permutation(T)[:S])
    d["xs_words"], d["xs_scales"] = pack_weight(n((K, S)) * s, "e4m3")
    d["w1"] = (n((K, H)) * 1.4 / K ** 0.5 / s).astype(np.float32)
    d["b1"] = (0.6 * n(H)).astype(np.float32)
    d["gain"] = (np.exp(0.3 * n(H)) * u[:, 0]).astype(np.float32)
    d["w2_words"], d["w2_scales"] = pack_weight(n((H, R)) * 1.3 / H ** 0.5 / u * u2.T, "e2m1")
    d["wx"] = (n((K, R)) / K ** 0.5 / s * u2.T).astype(np.float32)
    d["wo"] = (n((R, N)) / R ** 0.5 / u2).astype(np.float32)
    d["floor_n"] = (0.8 * n(N)).astype(np.float32)
    return d

def reference(tab_words, tab_scales, offs, xs_words, xs_scales, w1, b1, gain, w2_words, w2_scales, wx, wo, floor_n):
    v = unpack_weight(tab_words, tab_scales, "e4m3")[:, unstriped(offs)]
    xs = unpack_weight(xs_words, xs_scales, "e4m3")
    lin = mxq(f64(w1), 0, "e4m3").T @ v
    h = np.tanh(lin + f64(b1)[:, None]) * f64(gain)[:, None]
    w2 = unpack_weight(w2_words, w2_scales, "e2m1")
    expect = w2.T @ mxq(h, 0, "e4m3")
    seen = mxq(f64(wx), 0, "e4m3").T @ xs
    z = np.abs(expect - seen)
    y = mxq(f64(wo), 0, "e4m3").T @ mxq(z, 0, "e4m3")
    return np.maximum(y, f64(floor_n)[:, None])

@@ -1,0 +1,328 @@
+from contextlib import ExitStack
+
+import concourse.mybir as mybir
+
+K, T, S, H, R, N = 1024, 4096, 1024, 512, 1024, 384
+FLOPS = 2 * S * (K * H + H * R + K * R + R * N)
+
+F32 = mybir.dt.float32
+BF16 = mybir.dt.bfloat16
+I32 = mybir.dt.int32
+U32 = mybir.dt.uint32
+U16 = mybir.dt.uint16
+U8 = mybir.dt.uint8
+FP8X4 = mybir.dt.float8_e4m3fn_x4
+FP4X4 = mybir.dt.float4_e2m1fn_x4
+ACT = mybir.ActivationFunctionType
+ALU = mybir.AluOpType
+
+P = 128
+PACK = 4
+K_PASS = P * PACK
+BANK = 512
+HALF = 512
+QUARTER = 256
+
+
+def tile_list_sprouting_alarm_scores_kernel(
+    tc, tab_words, tab_scales, offs, xs_words, xs_scales, w1, b1, gain, w2_words, w2_scales, wx, wo, floor_n, out
+):
+    nc = tc.nc
+    with ExitStack() as ctx:
+        keep = ctx.enter_context(tc.tile_pool(name="keep", bufs=1))
+        ring = ctx.enter_context(tc.tile_pool(name="ring", bufs=4))
+        psum = ctx.enter_context(tc.psum_pool(name="psum", bufs=8))
+
+        def kept(shape, dtype, name):
+            return keep.tile(shape, dtype, name=name, align_bytes=64)
+
+        def rounded(name):
+            return ring.tile([P, 2048], BF16, name=name, tag="rounded", align_bytes=64)
+
+        def bank(name):
+            return psum.tile([P, BANK], F32, name=name, tag="bank")
+
+        def quantize(codes, scales, values):
+            nc.vector.quantize_mx(out=codes.bitcast(FP8X4), scales=scales, in_=values)
+
+        def copy_on(engine, dst, src):
+            if engine == "scalar":
+                nc.scalar.copy(out=dst, in_=src)
+            else:
+                nc.vector.tensor_copy(out=dst, in_=src)
+
+        offsets = keep.tile([P, S // 16], U16, name="offsets")
+        nc.sync.dma_start(offsets[:], offs)
+
+        tab_plane = kept([P, T], U8, "tab_plane")
+        nc.vector.memset(tab_plane[:].bitcast(I32), 0)
+        w2_plane_raw = kept([P, R], U8, "w2_plane_raw")
+        xs_plane = kept([P, S], U8, "xs_plane")
+        nc.vector.memset(w2_plane_raw[:].bitcast(I32), 0)
+        nc.vector.memset(xs_plane[:].bitcast(I32), 0)
+
+        def load_plane(queue, plane, scales):
+            passes = scales.shape[0]
+            for quad in range(4):
+                queue.dma_start(
+                    out=plane[32 * quad : 32 * quad + 4 * passes, :].bitcast(I32),
+                    in_=scales[:, 4 * quad : 4 * quad + 4, :].bitcast(I32),
+                )
+
+        bias = keep.tile([P, PACK], F32, name="bias")
+        nc.sync.dma_start(out=bias[:], in_=b1.rearrange("(p t) -> p t", t=PACK))
+        gains = keep.tile([P, PACK], F32, name="gains")
+        nc.sync.dma_start(out=gains[:], in_=gain.rearrange("(p t) -> p t", t=PACK))
+
+        def load_rows(rows, name):
+            raw = kept([P, PACK, rows.shape[1]], F32, name)
+            nc.sync.dma_start(out=raw[:], in_=rows.rearrange("(p i) w -> p i w", i=PACK))
+            return raw
+
+        def load_words(words, name):
+            tile = kept([P, words.shape[1]], U32, name)
+            nc.sync.dma_start(out=tile[:].bitcast(I32), in_=words.rearrange("p c i -> p (c i)").bitcast(I32))
+            return tile
+
+        def load_table(a, pieces):
+            tile = kept([P, T], U32, f"tab{a}")
+            words = tab_words[a].rearrange("p c i -> p (c i)").bitcast(I32)
+            for lo in range(0, T, T // pieces):
+                nc.sync.dma_start(out=tile[:, lo : lo + T // pieces].bitcast(I32), in_=words[:, lo : lo + T // pieces])
+            return tile
+
+        tab = [load_table(0, 8)]
+        load_plane(nc.sync, tab_plane, tab_scales)
+        w1_raw = {}
+        for c in range(2):
+            w1_raw[0, c] = load_rows(w1[:K_PASS, c * H // 2 : (c + 1) * H // 2], f"w1_raw0{c}")
+        load_plane(nc.sync, w2_plane_raw, w2_scales)
+        tab.append(load_table(1, 1))
+        for c in range(2):
+            w1_raw[1, c] = load_rows(w1[K_PASS:, c * H // 2 : (c + 1) * H // 2], f"w1_raw1{c}")
+        load_plane(nc.sync, xs_plane, xs_scales)
+        wx_raw, xs = {}, {}
+
+        def load_xs(a, u):
+            xs[a, u] = load_words(xs_words[a, :, u * HALF : (u + 1) * HALF, :], f"xs{a}{u}")
+
+        wx_raw[0, 0] = load_rows(wx[0:K_PASS, 0:K_PASS], "wx_raw00")
+        load_xs(0, 0)
+        w2_raw = kept([P, 2 * R], U8, "w2_raw")
+        nc.sync.dma_start(out=w2_raw[:].bitcast(I32), in_=w2_words[0].bitcast(I32))
+        wx_raw[1, 0] = load_rows(wx[K_PASS:, 0:K_PASS], "wx_raw10")
+        load_xs(1, 0)
+        wx_raw[0, 1] = load_rows(wx[0:K_PASS, K_PASS:], "wx_raw01")
+        load_xs(0, 1)
+        load_xs(1, 1)
+        wx_raw[1, 1] = load_rows(wx[K_PASS:, K_PASS:], "wx_raw11")
+        floors = keep.tile([P, N // P], F32, name="floors")
+        with nc.allow_non_contiguous_dma(reason="one floor to a partition"):
+            nc.sync.dma_start(out=floors[:], in_=floor_n.rearrange("(u p) -> p u", p=P))
+        wo_raw = []
+        for b in range(2):
+            raw = kept([P, PACK, N], F32, f"wo_raw{b}")
+            rows = wo[K_PASS * b : K_PASS * (b + 1), :].rearrange("(g t i) n -> t g i n", t=PACK, i=4)
+            for t in range(PACK):
+                nc.sync.dma_start(out=raw[:, t, :], in_=rows[t])
+            wo_raw.append(raw)
+
+        w1_codes, w1_plane = [], []
+
+        def make_w1(a, engines):
+            values = rounded(f"w1_bf{a}")
+            dst = values[:].rearrange("p (t q i) -> p q i t", t=PACK, i=PACK)
+            for c in range(2):
+                src = w1_raw[a, c][:].rearrange("p i (q t) -> p q i t", t=PACK)
+                copy_on(engines[c], dst[:, c * P // 2 : (c + 1) * P // 2], src)
+            w1_codes.append(kept([P, H], U32, f"w1_codes{a}"))
+            w1_plane.append(kept([P, H], U8, f"w1_plane{a}"))
+            for lo in range(0, H, H // 2):
+                hi = lo + H // 2
+                quantize(w1_codes[a][:, lo:hi], w1_plane[a][:, lo:hi], values[:, PACK * lo : PACK * hi])
+
+        v_words = {}
+
+        def gather_words(a):
+            v_words[a] = kept([P, S], U32, f"v_words{a}")
+            nc.vector.tensor_copy(v_words[a][:], tab[a][:].indirect(offsets[:]))
+
+        minus_gain = keep.tile([P, PACK], F32, name="minus_gain")
+        nc.vector.tensor_scalar(out=minus_gain[:], in0=gains[:], scalar1=-1.0, scalar2=None, op0=ALU.mult)
+        gather_words(0)
+        v_plane = kept([P, S], U8, "v_plane")
+        nc.vector.tensor_copy(v_plane[:], tab_plane[:].indirect(offsets[:]))
+        make_w1(0, ("scalar", "scalar"))
+        w2_dealt = kept([P, 2 * R], U8, "w2_dealt")
+        w2_plane = kept([P, R], U8, "w2_plane")
+        nc.vector.tensor_copy(
+            out=w2_plane[:].bitcast(I32).rearrange("p (b t g) -> p b t g", b=2, t=PACK),
+            in_=w2_plane_raw[:].bitcast(I32).rearrange("p (b g t) -> p b t g", b=2, t=PACK),
+        )
+        gather_words(1)
+        make_w1(1, ("scalar", "vector"))
+
+        lin = {}
+        for a in range(2):
+            for q in range(4):
+                for pair in range(2):
+                    if a == 0:
+                        lin[q, pair] = bank(f"lin{q}{pair}")
+                    for e in range(2):
+                        t = 2 * pair + e
+                        cols = slice(q * QUARTER, (q + 1) * QUARTER)
+                        nc.tensor.matmul_mx(
+                            out=lin[q, pair][:, e * QUARTER : (e + 1) * QUARTER],
+                            lhsT=w1_codes[a][:, t * P : (t + 1) * P].bitcast(FP8X4),
+                            lhsT_scale=w1_plane[a][:, t * P : (t + 1) * P],
+                            rhs=v_words[a][:, cols].bitcast(FP8X4),
+                            rhs_scale=v_plane[4 * a :, cols],
+                            start=(a == 0 and e == 0),
+                            stop=(a == 1 and e == 1),
+                        )
+
+        bounded = []
+        for q in range(4):
+            bounded.append(ring.tile([P, PACK, QUARTER], F32, name=f"bounded{q}", tag="bounded", align_bytes=64))
+            for t in range(PACK):
+                nc.scalar.activation(
+                    out=bounded[q][:, t, :],
+                    in_=lin[q, t // 2][:, (t % 2) * QUARTER : (t % 2 + 1) * QUARTER],
+                    func=ACT.Tanh,
+                    bias=bias[:, t : t + 1],
+                )
+
+        h_codes, h_plane = [], []
+
+        def make_h(q):
+            values = ring.tile([P, PACK * QUARTER], BF16, name=f"h_bf{q}", tag="quarter", align_bytes=64)
+            nc.vector.tensor_tensor(
+                out=values[:].rearrange("p (c i t) -> p c t i", i=4, t=PACK),
+                in0=bounded[q][:].rearrange("p t (c i) -> p c t i", i=4),
+                in1=minus_gain[:].unsqueeze(1).unsqueeze(3).to_broadcast([P, QUARTER // 4, PACK, 4]),
+                op=ALU.mult,
+            )
+            h_codes.append(kept([P, QUARTER], U32, f"h_codes{q}"))
+            h_plane.append(kept([P, QUARTER], U8, f"h_plane{q}"))
+            quantize(h_codes[q][:], h_plane[q][:], values[:])
+
+        wx_codes, wx_plane = {}, {}
+
+        def make_wx(a, b, engines):
+            values = rounded(f"wx_bf{a}{b}")
+            dst = values[:].rearrange("p (t g i j) -> p t g j i", t=PACK, i=4, j=PACK)
+            src = wx_raw[a, b][:].rearrange("p j (g t i) -> p t g j i", t=PACK, i=4)
+            for u in range(2):
+                copy_on(engines[u], dst[:, 2 * u : 2 * u + 2], src[:, 2 * u : 2 * u + 2])
+            wx_codes[a, b] = kept([P, K_PASS], U32, f"wx_codes{a}{b}")
+            wx_plane[a, b] = kept([P, K_PASS], U8, f"wx_plane{a}{b}")
+            quantize(wx_codes[a, b][:], wx_plane[a, b][:], values[:])
+
+        wo_codes, wo_plane = [], []
+
+        def make_wo(b, engine):
+            values = rounded(f"wo_bf{b}")
+            copy_on(
+                engine,
+                values[:, : PACK * N].rearrange("p (c i t) -> p c t i", i=4, t=PACK),
+                wo_raw[b][:].rearrange("p t (c i) -> p c t i", i=4),
+            )
+            wo_codes.append(kept([P, N], U32, f"wo_codes{b}"))
+            wo_plane.append(kept([P, N], U8, f"wo_plane{b}"))
+            for lo, hi in ((0, 2 * P), (2 * P, N)):
+                quantize(wo_codes[b][:, lo:hi], wo_plane[b][:, lo:hi], values[:, PACK * lo : PACK * hi])
+
+        z_values, z_codes, z_plane = {}, {}, {}
+
+        def make_z(b, q, expect_at):
+            values = kept([P, PACK * QUARTER], BF16, f"z_bf{b}{q}")
+            z_values[b, q] = values
+            for e in range(2):
+                acc = bank(f"diff{b}{q}{e}")
+                cols = slice(q * QUARTER + e * P, q * QUARTER + (e + 1) * P)
+                for step in range(3):
+                    for t in range(PACK):
+                        if step == expect_at:
+                            lo = b * K_PASS + t * P
+                            operands = dict(
+                                lhsT=w2_dealt[:, 2 * lo : 2 * (lo + P)].bitcast(FP4X4),
+                                lhsT_scale=w2_plane[:, lo : lo + P],
+                                rhs=h_codes[q][:, e * P : (e + 1) * P].bitcast(FP8X4),
+                                rhs_scale=h_plane[q][:, e * P : (e + 1) * P],
+                            )
+                        else:
+                            a = step - (step > expect_at)
+                            operands = dict(
+                                lhsT=wx_codes[a, b][:, t * P : (t + 1) * P].bitcast(FP8X4),
+                                lhsT_scale=wx_plane[a, b][:, t * P : (t + 1) * P],
+                                rhs=xs[a, q // 2][:, cols.start % HALF : cols.start % HALF + P].bitcast(FP8X4),
+                                rhs_scale=xs_plane[4 * a :, cols],
+                            )
+                        nc.tensor.matmul_mx(
+                            out=acc[:, t * P : (t + 1) * P],
+                            start=(step == 0 and t == 0),
+                            stop=(step == 2 and t == PACK - 1),
+                            **operands,
+                        )
+                nc.scalar.activation(
+                    out=values[:, e * BANK : (e + 1) * BANK].rearrange("p (j t) -> p j t", t=PACK),
+                    in_=acc[:].rearrange("p (t j) -> p j t", t=PACK),
+                    func=ACT.Abs,
+                )
+
+        def quantize_z(b, q):
+            z_codes[b, q] = kept([P, QUARTER], U32, f"z_codes{b}{q}")
+            z_plane[b, q] = kept([P, QUARTER], U8, f"z_plane{b}{q}")
+            quantize(z_codes[b, q][:], z_plane[b, q][:], z_values[b, q][:])
+
+        def make_scores(q):
+            scores = ring.tile([P, N // P, QUARTER], F32, name=f"scores{q}", tag="scores", align_bytes=64)
+            for u in range(N // P):
+                acc = bank(f"y{q}{u}")
+                for b in range(2):
+                    nc.tensor.matmul_mx(
+                        out=acc[:, :QUARTER],
+                        lhsT=wo_codes[b][:, u * P : (u + 1) * P].bitcast(FP8X4),
+                        lhsT_scale=wo_plane[b][:, u * P : (u + 1) * P],
+                        rhs=z_codes[b, q][:].bitcast(FP8X4),
+                        rhs_scale=z_plane[b, q][:],
+                        start=(b == 0),
+                        stop=(b == 1),
+                    )
+                nc.vector.tensor_scalar(
+                    out=scores[:, u, :], in0=acc[:, :QUARTER], scalar1=floors[:, u : u + 1], scalar2=None, op0=ALU.max
+                )
+                if q == 3:
+                    nc.sync.dma_start(out=out[u * P : (u + 1) * P, q * QUARTER :], in_=scores[:, u, :])
+            if q < 3:
+                nc.sync.dma_start(
+                    out=out[:, q * QUARTER : (q + 1) * QUARTER].rearrange("(u p) j -> p u j", p=P), in_=scores[:]
+                )
+
+        make_wx(0, 0, ("vector", "vector"))
+        make_h(0)
+        nc.vector.tensor_copy(
+            out=w2_dealt[:].bitcast(I32).rearrange("p (b t g w) -> p b t g w", b=2, t=PACK, w=2),
+            in_=w2_raw[:].bitcast(I32).rearrange("p (b g t w) -> p b t g w", b=2, t=PACK, w=2),
+        )
+        make_wx(1, 0, ("scalar", "vector"))
+        make_h(1)
+        make_z(0, 0, 1)
+        make_wx(0, 1, ("scalar", "vector"))
+        make_z(0, 1, 1)
+        make_h(2)
+        make_wx(1, 1, ("scalar", "vector"))
+        make_h(3)
+        make_z(1, 0, 0)
+        make_z(1, 1, 0)
+        make_z(0, 2, 2)
+        make_z(0, 3, 2)
+        make_wo(0, "vector")
+        make_wo(1, "scalar")
+        make_z(1, 2, 0)
+        for q in range(4):
+            if q == 1:
+                make_z(1, 3, 0)
+            quantize_z(0, q)
+            quantize_z(1, q)
+            make_scores(q)

@@ -31,7 +31,7 @@ def tile_list_sprouting_alarm_scores_kernel(
     with ExitStack() as ctx:
         keep = ctx.enter_context(tc.tile_pool(name="keep", bufs=1))
         ring = ctx.enter_context(tc.tile_pool(name="ring", bufs=4))
-        psum = ctx.enter_context(tc.psum_pool(name="psum", bufs=8))
+        psum = ctx.enter_context(tc.psum_pool(name="psum", bufs=1))
 
         def kept(shape, dtype, name):
             return keep.tile(shape, dtype, name=name, align_bytes=64)
@@ -39,8 +39,8 @@ def tile_list_sprouting_alarm_scores_kernel(
         def rounded(name):
             return ring.tile([P, 2048], BF16, name=name, tag="rounded", align_bytes=64)
 
-        def bank(name):
-            return psum.tile([P, BANK], F32, name=name, tag="bank")
+        def bank(index, name):
+            return psum.tile([P, BANK], F32, name=name, tag=f"bank{index}")
 
         def quantize(codes, scales, values):
             nc.vector.quantize_mx(out=codes.bitcast(FP8X4), scales=scales, in_=values)
@@ -84,23 +84,21 @@ def tile_list_sprouting_alarm_scores_kernel(
             nc.sync.dma_start(out=tile[:].bitcast(I32), in_=words.rearrange("p c i -> p (c i)").bitcast(I32))
             return tile
 
-        def load_table(a, pieces):
-            tile = kept([P, T], U32, f"tab{a}")
-            words = tab_words[a].rearrange("p c i -> p (c i)").bitcast(I32)
-            for lo in range(0, T, T // pieces):
-                nc.sync.dma_start(out=tile[:, lo : lo + T // pieces].bitcast(I32), in_=words[:, lo : lo + T // pieces])
-            return tile
+        def load_table_scales(a):
+            for quad in range(4):
+                nc.sync.dma_start(
+                    out=tab_plane[32 * quad + 4 * a : 32 * quad + 4 * a + 4, :].bitcast(I32),
+                    in_=tab_scales[a, 4 * quad : 4 * quad + 4, :].bitcast(I32),
+                )
 
-        tab = [load_table(0, 8)]
-        load_plane(nc.sync, tab_plane, tab_scales)
-        w1_raw = {}
-        for c in range(2):
-            w1_raw[0, c] = load_rows(w1[:K_PASS, c * H // 2 : (c + 1) * H // 2], f"w1_raw0{c}")
+        tab = [load_words(tab_words[0], "tab0")]
+        load_table_scales(0)
+        w1_raw = [load_rows(w1[:K_PASS, :], "w1_raw0")]
+        load_table_scales(1)
+        tab.append(load_words(tab_words[1], "tab1"))
         load_plane(nc.sync, w2_plane_raw, w2_scales)
-        tab.append(load_table(1, 1))
-        for c in range(2):
-            w1_raw[1, c] = load_rows(w1[K_PASS:, c * H // 2 : (c + 1) * H // 2], f"w1_raw1{c}")
-        load_plane(nc.sync, xs_plane, xs_scales)
+        w1_raw.append(load_rows(w1[K_PASS:, :], "w1_raw1"))
+        load_plane(nc.gpsimd, xs_plane, xs_scales)
         wx_raw, xs = {}, {}
 
         def load_xs(a, u):
@@ -116,25 +114,25 @@ def tile_list_sprouting_alarm_scores_kernel(
         load_xs(0, 1)
         load_xs(1, 1)
         wx_raw[1, 1] = load_rows(wx[K_PASS:, K_PASS:], "wx_raw11")
-        floors = keep.tile([P, N // P], F32, name="floors")
-        with nc.allow_non_contiguous_dma(reason="one floor to a partition"):
-            nc.sync.dma_start(out=floors[:], in_=floor_n.rearrange("(u p) -> p u", p=P))
         wo_raw = []
         for b in range(2):
-            raw = kept([P, PACK, N], F32, f"wo_raw{b}")
+            raw = keep.tile([P, PACK, N], F32, name=f"wo_raw{b}", tag=f"wo_raw{b}", align_bytes=64)
             rows = wo[K_PASS * b : K_PASS * (b + 1), :].rearrange("(g t i) n -> t g i n", t=PACK, i=4)
             for t in range(PACK):
                 nc.sync.dma_start(out=raw[:, t, :], in_=rows[t])
             wo_raw.append(raw)
+        floors = keep.tile([P, N // P], F32, name="floors")
+        with nc.allow_non_contiguous_dma(reason="one floor to a partition"):
+            nc.sync.dma_start(out=floors[:], in_=floor_n.rearrange("(u p) -> p u", p=P))
 
         w1_codes, w1_plane = [], []
 
-        def make_w1(a, engines):
+        def make_w1(a, split):
             values = rounded(f"w1_bf{a}")
             dst = values[:].rearrange("p (t q i) -> p q i t", t=PACK, i=PACK)
-            for c in range(2):
-                src = w1_raw[a, c][:].rearrange("p i (q t) -> p q i t", t=PACK)
-                copy_on(engines[c], dst[:, c * P // 2 : (c + 1) * P // 2], src)
+            src = w1_raw[a][:].rearrange("p i (q t) -> p q i t", t=PACK)
+            nc.scalar.copy(out=dst[:, :split], in_=src[:, :split])
+            nc.vector.tensor_copy(out=dst[:, split:], in_=src[:, split:])
             w1_codes.append(kept([P, H], U32, f"w1_codes{a}"))
             w1_plane.append(kept([P, H], U8, f"w1_plane{a}"))
             for lo in range(0, H, H // 2):
@@ -152,7 +150,7 @@ def tile_list_sprouting_alarm_scores_kernel(
         gather_words(0)
         v_plane = kept([P, S], U8, "v_plane")
         nc.vector.tensor_copy(v_plane[:], tab_plane[:].indirect(offsets[:]))
-        make_w1(0, ("scalar", "scalar"))
+        make_w1(0, 48)
         w2_dealt = kept([P, 2 * R], U8, "w2_dealt")
         w2_plane = kept([P, R], U8, "w2_plane")
         nc.vector.tensor_copy(
@@ -160,14 +158,14 @@ def tile_list_sprouting_alarm_scores_kernel(
             in_=w2_plane_raw[:].bitcast(I32).rearrange("p (b g t) -> p b t g", b=2, t=PACK),
         )
         gather_words(1)
-        make_w1(1, ("scalar", "vector"))
+        make_w1(1, 48)
 
         lin = {}
         for a in range(2):
             for q in range(4):
                 for pair in range(2):
                     if a == 0:
-                        lin[q, pair] = bank(f"lin{q}{pair}")
+                        lin[q, pair] = bank(2 * q + pair, f"lin{q}{pair}")
                     for e in range(2):
                         t = 2 * pair + e
                         cols = slice(q * QUARTER, (q + 1) * QUARTER)
@@ -196,11 +194,18 @@ def tile_list_sprouting_alarm_scores_kernel(
 
         def make_h(q):
             values = ring.tile([P, PACK * QUARTER], BF16, name=f"h_bf{q}", tag="quarter", align_bytes=64)
-            nc.vector.tensor_tensor(
+            gained = ring.tile([P, PACK, QUARTER], BF16, name=f"gained{q}", tag="gained", align_bytes=64)
+            for t in range(PACK):
+                nc.vector.tensor_scalar(
+                    out=gained[:, t, :],
+                    in0=bounded[q][:, t, :],
+                    scalar1=minus_gain[:, t : t + 1],
+                    scalar2=None,
+                    op0=ALU.mult,
+                )
+            nc.vector.tensor_copy(
                 out=values[:].rearrange("p (c i t) -> p c t i", i=4, t=PACK),
-                in0=bounded[q][:].rearrange("p t (c i) -> p c t i", i=4),
-                in1=minus_gain[:].unsqueeze(1).unsqueeze(3).to_broadcast([P, QUARTER // 4, PACK, 4]),
-                op=ALU.mult,
+                in_=gained[:].rearrange("p t (c i) -> p c t i", i=4),
             )
             h_codes.append(kept([P, QUARTER], U32, f"h_codes{q}"))
             h_plane.append(kept([P, QUARTER], U8, f"h_plane{q}"))
@@ -221,7 +226,7 @@ def tile_list_sprouting_alarm_scores_kernel(
         wo_codes, wo_plane = [], []
 
         def make_wo(b, engine):
-            values = rounded(f"wo_bf{b}")
+            values = keep.tile([P, PACK * N], BF16, name=f"wo_bf{b}", tag=f"wo_bf{b}", align_bytes=64)
             copy_on(
                 engine,
                 values[:, : PACK * N].rearrange("p (c i t) -> p c t i", i=4, t=PACK),
@@ -232,13 +237,14 @@ def tile_list_sprouting_alarm_scores_kernel(
             for lo, hi in ((0, 2 * P), (2 * P, N)):
                 quantize(wo_codes[b][:, lo:hi], wo_plane[b][:, lo:hi], values[:, PACK * lo : PACK * hi])
 
-        z_values, z_codes, z_plane = {}, {}, {}
+        z_values, z_tiles, z_codes, z_plane = {}, {}, {}, {}
 
         def make_z(b, q, expect_at):
-            values = kept([P, PACK * QUARTER], BF16, f"z_bf{b}{q}")
+            tag = "wo_raw1" if (b, q) == (1, 0) else f"z_bf{b}{q}"
+            values = keep.tile([P, PACK * QUARTER], BF16, name=f"z_bf{b}{q}", tag=tag, align_bytes=64)
             z_values[b, q] = values
             for e in range(2):
-                acc = bank(f"diff{b}{q}{e}")
+                acc = bank(2 * (q % 2) + (4 * b if q < 2 else 0) + e, f"diff{b}{q}{e}")
                 cols = slice(q * QUARTER + e * P, q * QUARTER + (e + 1) * P)
                 for step in range(3):
                     for t in range(PACK):
@@ -271,26 +277,33 @@ def tile_list_sprouting_alarm_scores_kernel(
                 )
 
         def quantize_z(b, q):
-            z_codes[b, q] = kept([P, QUARTER], U32, f"z_codes{b}{q}")
+            key = (b, q // 2) if b == 0 else (1, 0)
+            if key not in z_tiles:
+                tag = {(0, 0): "z_first", (0, 1): "wo_bf0", (1, 0): "wo_bf1"}[key]
+                z_tiles[key] = keep.tile([P, HALF * (b + 1)], U32, name=f"z_codes{b}{q}", tag=tag, align_bytes=64)
+            lo = (q % 2 if b == 0 else q) * QUARTER
+            z_codes[b, q] = z_tiles[key][:, lo : lo + QUARTER]
             z_plane[b, q] = kept([P, QUARTER], U8, f"z_plane{b}{q}")
-            quantize(z_codes[b, q][:], z_plane[b, q][:], z_values[b, q][:])
+            quantize(z_codes[b, q], z_plane[b, q][:], z_values[b, q][:])
 
         def make_scores(q):
             scores = ring.tile([P, N // P, QUARTER], F32, name=f"scores{q}", tag="scores", align_bytes=64)
+            banks = [bank((4 + 2 * q + e) % 8, f"y{q}{e}") for e in range(2)]
+            sums = [banks[u // 2][:, (u % 2) * QUARTER : (u % 2 + 1) * QUARTER] for u in range(N // P)]
             for u in range(N // P):
-                acc = bank(f"y{q}{u}")
                 for b in range(2):
                     nc.tensor.matmul_mx(
-                        out=acc[:, :QUARTER],
+                        out=sums[u],
                         lhsT=wo_codes[b][:, u * P : (u + 1) * P].bitcast(FP8X4),
                         lhsT_scale=wo_plane[b][:, u * P : (u + 1) * P],
-                        rhs=z_codes[b, q][:].bitcast(FP8X4),
+                        rhs=z_codes[b, q].bitcast(FP8X4),
                         rhs_scale=z_plane[b, q][:],
                         start=(b == 0),
                         stop=(b == 1),
                     )
+            for u in range(N // P):
                 nc.vector.tensor_scalar(
-                    out=scores[:, u, :], in0=acc[:, :QUARTER], scalar1=floors[:, u : u + 1], scalar2=None, op0=ALU.max
+                    out=scores[:, u, :], in0=sums[u], scalar1=floors[:, u : u + 1], scalar2=None, op0=ALU.max
                 )
                 if q == 3:
                     nc.sync.dma_start(out=out[u * P : (u + 1) * P, q * QUARTER :], in_=scores[:, u, :])
@@ -308,21 +321,21 @@ def tile_list_sprouting_alarm_scores_kernel(
         make_wx(1, 0, ("scalar", "vector"))
         make_h(1)
         make_z(0, 0, 1)
-        make_wx(0, 1, ("scalar", "vector"))
         make_z(0, 1, 1)
+        make_wx(0, 1, ("scalar", "vector"))
         make_h(2)
+        make_z(0, 2, 2)
         make_wx(1, 1, ("scalar", "vector"))
         make_h(3)
-        make_z(1, 0, 0)
-        make_z(1, 1, 0)
-        make_z(0, 2, 2)
         make_z(0, 3, 2)
         make_wo(0, "vector")
         make_wo(1, "scalar")
-        make_z(1, 2, 0)
+        make_z(1, 0, 0)
+        make_z(1, 1, 0)
+        make_z(1, 2, 1)
         for q in range(4):
             if q == 1:
-                make_z(1, 3, 0)
+                make_z(1, 3, 1)
             quantize_z(0, q)
             quantize_z(1, q)
             make_scores(q)

@@ -17,11 +17,14 @@ ACT = mybir.ActivationFunctionType
 ALU = mybir.AluOpType
 
 P = 128
-PACK = 4
-K_PASS = P * PACK
+SLOTS = 4
+K_PASS = P * SLOTS
+RUN = 4
 BANK = 512
-HALF = 512
-QUARTER = 256
+HALF = S // 2
+QUARTER = S // 4
+SCORE_TILES = N // P
+W1_SCALAR_SHARE = 48
 
 
 def tile_list_sprouting_alarm_scores_kernel(
@@ -33,23 +36,14 @@ def tile_list_sprouting_alarm_scores_kernel(
         ring = ctx.enter_context(tc.tile_pool(name="ring", bufs=4))
         psum = ctx.enter_context(tc.psum_pool(name="psum", bufs=1))
 
-        def kept(shape, dtype, name):
-            return keep.tile(shape, dtype, name=name, align_bytes=64)
-
-        def rounded(name):
-            return ring.tile([P, 2048], BF16, name=name, tag="rounded", align_bytes=64)
+        def kept(shape, dtype, name, room=None):
+            return keep.tile(shape, dtype, name=name, tag=room or name, align_bytes=64)
 
         def bank(index, name):
             return psum.tile([P, BANK], F32, name=name, tag=f"bank{index}")
 
-        def quantize(codes, scales, values):
-            nc.vector.quantize_mx(out=codes.bitcast(FP8X4), scales=scales, in_=values)
-
-        def copy_on(engine, dst, src):
-            if engine == "scalar":
-                nc.scalar.copy(out=dst, in_=src)
-            else:
-                nc.vector.tensor_copy(out=dst, in_=src)
+        def quantize(codes, plane, values):
+            nc.vector.quantize_mx(out=codes.bitcast(FP8X4), scales=plane, in_=values)
 
         offsets = keep.tile([P, S // 16], U16, name="offsets")
         nc.sync.dma_start(offsets[:], offs)
@@ -69,27 +63,27 @@ def tile_list_sprouting_alarm_scores_kernel(
                     in_=scales[:, 4 * quad : 4 * quad + 4, :].bitcast(I32),
                 )
 
-        bias = keep.tile([P, PACK], F32, name="bias")
-        nc.sync.dma_start(out=bias[:], in_=b1.rearrange("(p t) -> p t", t=PACK))
-        gains = keep.tile([P, PACK], F32, name="gains")
-        nc.sync.dma_start(out=gains[:], in_=gain.rearrange("(p t) -> p t", t=PACK))
-
-        def load_rows(rows, name):
-            raw = kept([P, PACK, rows.shape[1]], F32, name)
-            nc.sync.dma_start(out=raw[:], in_=rows.rearrange("(p i) w -> p i w", i=PACK))
-            return raw
-
-        def load_words(words, name):
-            tile = kept([P, words.shape[1]], U32, name)
-            nc.sync.dma_start(out=tile[:].bitcast(I32), in_=words.rearrange("p c i -> p (c i)").bitcast(I32))
-            return tile
-
         def load_table_scales(a):
             for quad in range(4):
                 nc.sync.dma_start(
                     out=tab_plane[32 * quad + 4 * a : 32 * quad + 4 * a + 4, :].bitcast(I32),
                     in_=tab_scales[a, 4 * quad : 4 * quad + 4, :].bitcast(I32),
                 )
+
+        def load_rows(rows, name):
+            raw = kept([P, SLOTS, rows.shape[1]], F32, name)
+            nc.sync.dma_start(out=raw[:], in_=rows.rearrange("(p j) w -> p j w", j=SLOTS))
+            return raw
+
+        def load_words(words, name):
+            tile = kept([P, words.shape[1]], U32, name)
+            nc.sync.dma_start(out=tile[:].bitcast(I32), in_=words.rearrange("p c j -> p (c j)").bitcast(I32))
+            return tile
+
+        bias = keep.tile([P, SLOTS], F32, name="bias")
+        nc.sync.dma_start(out=bias[:], in_=b1.rearrange("(p t) -> p t", t=SLOTS))
+        gains = keep.tile([P, SLOTS], F32, name="gains")
+        nc.sync.dma_start(out=gains[:], in_=gain.rearrange("(p t) -> p t", t=SLOTS))
 
         tab = [load_words(tab_words[0], "tab0")]
         load_table_scales(0)
@@ -99,45 +93,49 @@ def tile_list_sprouting_alarm_scores_kernel(
         load_plane(nc.sync, w2_plane_raw, w2_scales)
         w1_raw.append(load_rows(w1[K_PASS:, :], "w1_raw1"))
         load_plane(nc.gpsimd, xs_plane, xs_scales)
+
         wx_raw, xs = {}, {}
 
-        def load_xs(a, u):
-            xs[a, u] = load_words(xs_words[a, :, u * HALF : (u + 1) * HALF, :], f"xs{a}{u}")
+        def load_wx(a, b):
+            wx_raw[a, b] = load_rows(wx[K_PASS * a : K_PASS * (a + 1), K_PASS * b : K_PASS * (b + 1)], f"wx_raw{a}{b}")
 
-        wx_raw[0, 0] = load_rows(wx[0:K_PASS, 0:K_PASS], "wx_raw00")
+        def load_xs(a, half):
+            xs[a, half] = load_words(xs_words[a, :, half * HALF : (half + 1) * HALF, :], f"xs{a}{half}")
+
+        load_wx(0, 0)
         load_xs(0, 0)
         w2_raw = kept([P, 2 * R], U8, "w2_raw")
         nc.sync.dma_start(out=w2_raw[:].bitcast(I32), in_=w2_words[0].bitcast(I32))
-        wx_raw[1, 0] = load_rows(wx[K_PASS:, 0:K_PASS], "wx_raw10")
+        load_wx(1, 0)
         load_xs(1, 0)
-        wx_raw[0, 1] = load_rows(wx[0:K_PASS, K_PASS:], "wx_raw01")
+        load_wx(0, 1)
         load_xs(0, 1)
         load_xs(1, 1)
-        wx_raw[1, 1] = load_rows(wx[K_PASS:, K_PASS:], "wx_raw11")
+        load_wx(1, 1)
         wo_raw = []
         for b in range(2):
-            raw = keep.tile([P, PACK, N], F32, name=f"wo_raw{b}", tag=f"wo_raw{b}", align_bytes=64)
-            rows = wo[K_PASS * b : K_PASS * (b + 1), :].rearrange("(g t i) n -> t g i n", t=PACK, i=4)
-            for t in range(PACK):
+            raw = kept([P, SLOTS, N], F32, f"wo_raw{b}")
+            rows = wo[K_PASS * b : K_PASS * (b + 1), :].rearrange("(g t i) n -> t g i n", t=SLOTS, i=RUN)
+            for t in range(SLOTS):
                 nc.sync.dma_start(out=raw[:, t, :], in_=rows[t])
             wo_raw.append(raw)
-        floors = keep.tile([P, N // P], F32, name="floors")
+        floors = keep.tile([P, SCORE_TILES], F32, name="floors")
         with nc.allow_non_contiguous_dma(reason="one floor to a partition"):
             nc.sync.dma_start(out=floors[:], in_=floor_n.rearrange("(u p) -> p u", p=P))
 
         w1_codes, w1_plane = [], []
 
-        def make_w1(a, split):
-            values = rounded(f"w1_bf{a}")
-            dst = values[:].rearrange("p (t q i) -> p q i t", t=PACK, i=PACK)
-            src = w1_raw[a][:].rearrange("p i (q t) -> p q i t", t=PACK)
-            nc.scalar.copy(out=dst[:, :split], in_=src[:, :split])
-            nc.vector.tensor_copy(out=dst[:, split:], in_=src[:, split:])
+        def make_w1(a):
+            values = ring.tile([P, SLOTS * H], BF16, name=f"w1_bf{a}", tag="rounded", align_bytes=64)
+            dst = values[:].rearrange("p (t c j) -> p c j t", t=SLOTS, j=SLOTS)
+            src = w1_raw[a][:].rearrange("p j (c t) -> p c j t", t=SLOTS)
+            nc.scalar.copy(out=dst[:, :W1_SCALAR_SHARE], in_=src[:, :W1_SCALAR_SHARE])
+            nc.vector.tensor_copy(out=dst[:, W1_SCALAR_SHARE:], in_=src[:, W1_SCALAR_SHARE:])
             w1_codes.append(kept([P, H], U32, f"w1_codes{a}"))
             w1_plane.append(kept([P, H], U8, f"w1_plane{a}"))
             for lo in range(0, H, H // 2):
                 hi = lo + H // 2
-                quantize(w1_codes[a][:, lo:hi], w1_plane[a][:, lo:hi], values[:, PACK * lo : PACK * hi])
+                quantize(w1_codes[a][:, lo:hi], w1_plane[a][:, lo:hi], values[:, SLOTS * lo : SLOTS * hi])
 
         v_words = {}
 
@@ -145,20 +143,20 @@ def tile_list_sprouting_alarm_scores_kernel(
             v_words[a] = kept([P, S], U32, f"v_words{a}")
             nc.vector.tensor_copy(v_words[a][:], tab[a][:].indirect(offsets[:]))
 
-        minus_gain = keep.tile([P, PACK], F32, name="minus_gain")
+        minus_gain = keep.tile([P, SLOTS], F32, name="minus_gain")
         nc.vector.tensor_scalar(out=minus_gain[:], in0=gains[:], scalar1=-1.0, scalar2=None, op0=ALU.mult)
         gather_words(0)
         v_plane = kept([P, S], U8, "v_plane")
         nc.vector.tensor_copy(v_plane[:], tab_plane[:].indirect(offsets[:]))
-        make_w1(0, 48)
+        make_w1(0)
         w2_dealt = kept([P, 2 * R], U8, "w2_dealt")
         w2_plane = kept([P, R], U8, "w2_plane")
         nc.vector.tensor_copy(
-            out=w2_plane[:].bitcast(I32).rearrange("p (b t g) -> p b t g", b=2, t=PACK),
-            in_=w2_plane_raw[:].bitcast(I32).rearrange("p (b g t) -> p b t g", b=2, t=PACK),
+            out=w2_plane[:].bitcast(I32).rearrange("p (b t g) -> p b t g", b=2, t=SLOTS),
+            in_=w2_plane_raw[:].bitcast(I32).rearrange("p (b g t) -> p b t g", b=2, t=SLOTS),
         )
         gather_words(1)
-        make_w1(1, 48)
+        make_w1(1)
 
         lin = {}
         for a in range(2):
@@ -166,23 +164,22 @@ def tile_list_sprouting_alarm_scores_kernel(
                 for pair in range(2):
                     if a == 0:
                         lin[q, pair] = bank(2 * q + pair, f"lin{q}{pair}")
-                    for e in range(2):
-                        t = 2 * pair + e
+                    for t in (2 * pair, 2 * pair + 1):
                         cols = slice(q * QUARTER, (q + 1) * QUARTER)
                         nc.tensor.matmul_mx(
-                            out=lin[q, pair][:, e * QUARTER : (e + 1) * QUARTER],
+                            out=lin[q, pair][:, (t % 2) * QUARTER : (t % 2 + 1) * QUARTER],
                             lhsT=w1_codes[a][:, t * P : (t + 1) * P].bitcast(FP8X4),
                             lhsT_scale=w1_plane[a][:, t * P : (t + 1) * P],
                             rhs=v_words[a][:, cols].bitcast(FP8X4),
                             rhs_scale=v_plane[4 * a :, cols],
-                            start=(a == 0 and e == 0),
-                            stop=(a == 1 and e == 1),
+                            start=(a == 0 and t % 2 == 0),
+                            stop=(a == 1 and t % 2 == 1),
                         )
 
         bounded = []
         for q in range(4):
-            bounded.append(ring.tile([P, PACK, QUARTER], F32, name=f"bounded{q}", tag="bounded", align_bytes=64))
-            for t in range(PACK):
+            bounded.append(ring.tile([P, SLOTS, QUARTER], F32, name=f"bounded{q}", tag="bounded", align_bytes=64))
+            for t in range(SLOTS):
                 nc.scalar.activation(
                     out=bounded[q][:, t, :],
                     in_=lin[q, t // 2][:, (t % 2) * QUARTER : (t % 2 + 1) * QUARTER],
@@ -193,19 +190,12 @@ def tile_list_sprouting_alarm_scores_kernel(
         h_codes, h_plane = [], []
 
         def make_h(q):
-            values = ring.tile([P, PACK * QUARTER], BF16, name=f"h_bf{q}", tag="quarter", align_bytes=64)
-            gained = ring.tile([P, PACK, QUARTER], BF16, name=f"gained{q}", tag="gained", align_bytes=64)
-            for t in range(PACK):
-                nc.vector.tensor_scalar(
-                    out=gained[:, t, :],
-                    in0=bounded[q][:, t, :],
-                    scalar1=minus_gain[:, t : t + 1],
-                    scalar2=None,
-                    op0=ALU.mult,
-                )
-            nc.vector.tensor_copy(
-                out=values[:].rearrange("p (c i t) -> p c t i", i=4, t=PACK),
-                in_=gained[:].rearrange("p t (c i) -> p c t i", i=4),
+            values = ring.tile([P, SLOTS * QUARTER], BF16, name=f"h_bf{q}", tag="h_rounded", align_bytes=64)
+            nc.vector.tensor_tensor(
+                out=values[:].rearrange("p (c i t) -> p c t i", i=RUN, t=SLOTS),
+                in0=bounded[q][:].rearrange("p t (c i) -> p c t i", i=RUN),
+                in1=minus_gain[:].unsqueeze(1).unsqueeze(3).to_broadcast([P, QUARTER // RUN, SLOTS, RUN]),
+                op=ALU.mult,
             )
             h_codes.append(kept([P, QUARTER], U32, f"h_codes{q}"))
             h_plane.append(kept([P, QUARTER], U8, f"h_plane{q}"))
@@ -213,41 +203,44 @@ def tile_list_sprouting_alarm_scores_kernel(
 
         wx_codes, wx_plane = {}, {}
 
-        def make_wx(a, b, engines):
-            values = rounded(f"wx_bf{a}{b}")
-            dst = values[:].rearrange("p (t g i j) -> p t g j i", t=PACK, i=4, j=PACK)
-            src = wx_raw[a, b][:].rearrange("p j (g t i) -> p t g j i", t=PACK, i=4)
-            for u in range(2):
-                copy_on(engines[u], dst[:, 2 * u : 2 * u + 2], src[:, 2 * u : 2 * u + 2])
+        def make_wx(a, b, scalar_slots):
+            values = ring.tile([P, SLOTS * K_PASS], BF16, name=f"wx_bf{a}{b}", tag="rounded", align_bytes=64)
+            dst = values[:].rearrange("p (t g i j) -> p g t j i", t=SLOTS, i=RUN, j=SLOTS)
+            src = wx_raw[a, b][:].rearrange("p j (g t i) -> p g t j i", t=SLOTS, i=RUN)
+            if scalar_slots:
+                nc.scalar.copy(out=dst[:, :, :scalar_slots], in_=src[:, :, :scalar_slots])
+            nc.vector.tensor_copy(out=dst[:, :, scalar_slots:], in_=src[:, :, scalar_slots:])
             wx_codes[a, b] = kept([P, K_PASS], U32, f"wx_codes{a}{b}")
             wx_plane[a, b] = kept([P, K_PASS], U8, f"wx_plane{a}{b}")
             quantize(wx_codes[a, b][:], wx_plane[a, b][:], values[:])
 
         wo_codes, wo_plane = [], []
 
-        def make_wo(b, engine):
-            values = keep.tile([P, PACK * N], BF16, name=f"wo_bf{b}", tag=f"wo_bf{b}", align_bytes=64)
-            copy_on(
-                engine,
-                values[:, : PACK * N].rearrange("p (c i t) -> p c t i", i=4, t=PACK),
-                wo_raw[b][:].rearrange("p t (c i) -> p c t i", i=4),
+        def make_wo(b):
+            values = kept([P, SLOTS * N], BF16, f"wo_bf{b}")
+            nc.vector.tensor_copy(
+                out=values[:].rearrange("p (c i t) -> p c t i", i=RUN, t=SLOTS),
+                in_=wo_raw[b][:].rearrange("p t (c i) -> p c t i", i=RUN),
             )
             wo_codes.append(kept([P, N], U32, f"wo_codes{b}"))
             wo_plane.append(kept([P, N], U8, f"wo_plane{b}"))
             for lo, hi in ((0, 2 * P), (2 * P, N)):
-                quantize(wo_codes[b][:, lo:hi], wo_plane[b][:, lo:hi], values[:, PACK * lo : PACK * hi])
+                quantize(wo_codes[b][:, lo:hi], wo_plane[b][:, lo:hi], values[:, SLOTS * lo : SLOTS * hi])
 
-        z_values, z_tiles, z_codes, z_plane = {}, {}, {}, {}
+        z_rounded, z_values, z_tiles, z_codes, z_plane = {}, {}, {}, {}, {}
 
         def make_z(b, q, expect_at):
-            tag = "wo_raw1" if (b, q) == (1, 0) else f"z_bf{b}{q}"
-            values = keep.tile([P, PACK * QUARTER], BF16, name=f"z_bf{b}{q}", tag=tag, align_bytes=64)
+            key = (b, q // 2)
+            if q % 2 == 0:
+                room = "wx_raw11" if key == (0, 1) else None
+                z_rounded[key] = kept([P, SLOTS * HALF], BF16, f"z_bf{b}{q // 2}", room)
+            values = z_rounded[key][:, (q % 2) * SLOTS * QUARTER : (q % 2 + 1) * SLOTS * QUARTER]
             z_values[b, q] = values
             for e in range(2):
                 acc = bank(2 * (q % 2) + (4 * b if q < 2 else 0) + e, f"diff{b}{q}{e}")
                 cols = slice(q * QUARTER + e * P, q * QUARTER + (e + 1) * P)
                 for step in range(3):
-                    for t in range(PACK):
+                    for t in range(SLOTS):
                         if step == expect_at:
                             lo = b * K_PASS + t * P
                             operands = dict(
@@ -267,30 +260,35 @@ def tile_list_sprouting_alarm_scores_kernel(
                         nc.tensor.matmul_mx(
                             out=acc[:, t * P : (t + 1) * P],
                             start=(step == 0 and t == 0),
-                            stop=(step == 2 and t == PACK - 1),
+                            stop=(step == 2 and t == SLOTS - 1),
                             **operands,
                         )
                 nc.scalar.activation(
-                    out=values[:, e * BANK : (e + 1) * BANK].rearrange("p (j t) -> p j t", t=PACK),
-                    in_=acc[:].rearrange("p (t j) -> p j t", t=PACK),
+                    out=values[:, e * BANK : (e + 1) * BANK].rearrange("p (s t) -> p s t", t=SLOTS),
+                    in_=acc[:].rearrange("p (t s) -> p s t", t=SLOTS),
                     func=ACT.Abs,
                 )
 
         def quantize_z(b, q):
-            key = (b, q // 2) if b == 0 else (1, 0)
-            if key not in z_tiles:
-                tag = {(0, 0): "z_first", (0, 1): "wo_bf0", (1, 0): "wo_bf1"}[key]
-                z_tiles[key] = keep.tile([P, HALF * (b + 1)], U32, name=f"z_codes{b}{q}", tag=tag, align_bytes=64)
-            lo = (q % 2 if b == 0 else q) * QUARTER
-            z_codes[b, q] = z_tiles[key][:, lo : lo + QUARTER]
+            piece = 4 * b + q
+            room, first, count = ("z_early", 0, 2) if piece < 2 else ("wo_bf1", 2, 6)
+            if room not in z_tiles:
+                z_tiles[room] = kept([P, count * QUARTER], U32, f"z_codes{piece}", room)
+            z_codes[b, q] = z_tiles[room][:, (piece - first) * QUARTER : (piece - first + 1) * QUARTER]
             z_plane[b, q] = kept([P, QUARTER], U8, f"z_plane{b}{q}")
-            quantize(z_codes[b, q], z_plane[b, q][:], z_values[b, q][:])
+            quantize(z_codes[b, q], z_plane[b, q][:], z_values[b, q])
+
+        minus_floors = keep.tile([P, SCORE_TILES], F32, name="minus_floors")
 
         def make_scores(q):
-            scores = ring.tile([P, N // P, QUARTER], F32, name=f"scores{q}", tag="scores", align_bytes=64)
-            banks = [bank((4 + 2 * q + e) % 8, f"y{q}{e}") for e in range(2)]
-            sums = [banks[u // 2][:, (u % 2) * QUARTER : (u % 2 + 1) * QUARTER] for u in range(N // P)]
-            for u in range(N // P):
+            scores = ring.tile([P, SCORE_TILES, QUARTER], F32, name=f"scores{q}", tag="scores", align_bytes=64)
+            last = q == 3
+            if last:
+                sums = [bank(2 + u, f"y{q}{u}")[:, :QUARTER] for u in range(SCORE_TILES)]
+            else:
+                banks = [bank((4 + 2 * q + n) % 8, f"y{q}{n}") for n in range(2)]
+                sums = [banks[0][:, :QUARTER], banks[1][:, :QUARTER], banks[1][:, QUARTER:]]
+            for u in range(SCORE_TILES):
                 for b in range(2):
                     nc.tensor.matmul_mx(
                         out=sums[u],
@@ -301,41 +299,46 @@ def tile_list_sprouting_alarm_scores_kernel(
                         start=(b == 0),
                         stop=(b == 1),
                     )
-            for u in range(N // P):
-                nc.vector.tensor_scalar(
-                    out=scores[:, u, :], in0=sums[u], scalar1=floors[:, u : u + 1], scalar2=None, op0=ALU.max
-                )
-                if q == 3:
+            for u in range(SCORE_TILES):
+                floor = floors[:, u : u + 1]
+                if u == 0:
+                    above = ring.tile([P, QUARTER], F32, name=f"above{q}", tag="above")
+                    nc.scalar.activation(out=above[:], in_=sums[u], func=ACT.Relu, bias=minus_floors[:, u : u + 1])
+                    nc.scalar.activation(out=scores[:, u, :], in_=above[:], func=ACT.Identity, bias=floor)
+                else:
+                    nc.vector.tensor_scalar(out=scores[:, u, :], in0=sums[u], scalar1=floor, scalar2=None, op0=ALU.max)
+                if last:
                     nc.sync.dma_start(out=out[u * P : (u + 1) * P, q * QUARTER :], in_=scores[:, u, :])
-            if q < 3:
+            if not last:
                 nc.sync.dma_start(
-                    out=out[:, q * QUARTER : (q + 1) * QUARTER].rearrange("(u p) j -> p u j", p=P), in_=scores[:]
+                    out=out[:, q * QUARTER : (q + 1) * QUARTER].rearrange("(u p) s -> p u s", p=P), in_=scores[:]
                 )
 
-        make_wx(0, 0, ("vector", "vector"))
+        make_wx(0, 0, scalar_slots=0)
         make_h(0)
         nc.vector.tensor_copy(
-            out=w2_dealt[:].bitcast(I32).rearrange("p (b t g w) -> p b t g w", b=2, t=PACK, w=2),
-            in_=w2_raw[:].bitcast(I32).rearrange("p (b g t w) -> p b t g w", b=2, t=PACK, w=2),
+            out=w2_dealt[:].bitcast(I32).rearrange("p (b t g w) -> p b t g w", b=2, t=SLOTS, w=2),
+            in_=w2_raw[:].bitcast(I32).rearrange("p (b g t w) -> p b t g w", b=2, t=SLOTS, w=2),
         )
-        make_wx(1, 0, ("scalar", "vector"))
+        make_wx(1, 0, scalar_slots=2)
         make_h(1)
-        make_z(0, 0, 1)
-        make_z(0, 1, 1)
-        make_wx(0, 1, ("scalar", "vector"))
+        make_z(0, 0, expect_at=1)
+        make_z(0, 1, expect_at=1)
+        make_wx(0, 1, scalar_slots=2)
         make_h(2)
-        make_z(0, 2, 2)
-        make_wx(1, 1, ("scalar", "vector"))
+        make_wx(1, 1, scalar_slots=2)
+        make_z(0, 2, expect_at=2)
         make_h(3)
-        make_z(0, 3, 2)
-        make_wo(0, "vector")
-        make_wo(1, "scalar")
-        make_z(1, 0, 0)
-        make_z(1, 1, 0)
-        make_z(1, 2, 1)
+        make_z(0, 3, expect_at=2)
+        make_wo(0)
+        make_wo(1)
+        nc.vector.tensor_scalar(out=minus_floors[:], in0=floors[:], scalar1=-1.0, scalar2=None, op0=ALU.mult)
+        make_z(1, 0, expect_at=0)
+        make_z(1, 1, expect_at=0)
+        make_z(1, 2, expect_at=1)
         for q in range(4):
             if q == 1:
-                make_z(1, 3, 1)
+                make_z(1, 3, expect_at=1)
             quantize_z(0, q)
             quantize_z(1, q)
             make_scores(q)

from contextlib import ExitStack

import concourse.mybir as mybir

K, T, S, H, R, N = 1024, 4096, 1024, 512, 1024, 384
FLOPS = 2 * S * (K * H + H * R + K * R + R * N)

F32 = mybir.dt.float32
BF16 = mybir.dt.bfloat16
I32 = mybir.dt.int32
U32 = mybir.dt.uint32
U16 = mybir.dt.uint16
U8 = mybir.dt.uint8
FP8X4 = mybir.dt.float8_e4m3fn_x4
FP4X4 = mybir.dt.float4_e2m1fn_x4
ACT = mybir.ActivationFunctionType
ALU = mybir.AluOpType

P = 128
SLOTS = 4
K_PASS = P * SLOTS
RUN = 4
BANK = 512
HALF = S // 2
QUARTER = S // 4
SCORE_TILES = N // P
W1_SCALAR_SHARE = 48


def tile_list_sprouting_alarm_scores_kernel(
    tc, tab_words, tab_scales, offs, xs_words, xs_scales, w1, b1, gain, w2_words, w2_scales, wx, wo, floor_n, out
):
    nc = tc.nc
    with ExitStack() as ctx:
        keep = ctx.enter_context(tc.tile_pool(name="keep", bufs=1))
        ring = ctx.enter_context(tc.tile_pool(name="ring", bufs=4))
        psum = ctx.enter_context(tc.psum_pool(name="psum", bufs=1))

        def kept(shape, dtype, name, room=None):
            return keep.tile(shape, dtype, name=name, tag=room or name, align_bytes=64)

        def bank(index, name):
            return psum.tile([P, BANK], F32, name=name, tag=f"bank{index}")

        def quantize(codes, plane, values):
            nc.vector.quantize_mx(out=codes.bitcast(FP8X4), scales=plane, in_=values)

        offsets = keep.tile([P, S // 16], U16, name="offsets")
        nc.sync.dma_start(offsets[:], offs)

        tab_plane = kept([P, T], U8, "tab_plane")
        nc.vector.memset(tab_plane[:].bitcast(I32), 0)
        w2_plane_raw = kept([P, R], U8, "w2_plane_raw")
        xs_plane = kept([P, S], U8, "xs_plane")
        nc.vector.memset(w2_plane_raw[:].bitcast(I32), 0)
        nc.vector.memset(xs_plane[:].bitcast(I32), 0)

        def load_plane(queue, plane, scales):
            passes = scales.shape[0]
            for quad in range(4):
                queue.dma_start(
                    out=plane[32 * quad : 32 * quad + 4 * passes, :].bitcast(I32),
                    in_=scales[:, 4 * quad : 4 * quad + 4, :].bitcast(I32),
                )

        def load_table_scales(a):
            for quad in range(4):
                nc.sync.dma_start(
                    out=tab_plane[32 * quad + 4 * a : 32 * quad + 4 * a + 4, :].bitcast(I32),
                    in_=tab_scales[a, 4 * quad : 4 * quad + 4, :].bitcast(I32),
                )

        def load_rows(rows, name):
            raw = kept([P, SLOTS, rows.shape[1]], F32, name)
            nc.sync.dma_start(out=raw[:], in_=rows.rearrange("(p j) w -> p j w", j=SLOTS))
            return raw

        def load_words(words, name):
            tile = kept([P, words.shape[1]], U32, name)
            nc.sync.dma_start(out=tile[:].bitcast(I32), in_=words.rearrange("p c j -> p (c j)").bitcast(I32))
            return tile

        bias = keep.tile([P, SLOTS], F32, name="bias")
        nc.sync.dma_start(out=bias[:], in_=b1.rearrange("(p t) -> p t", t=SLOTS))
        gains = keep.tile([P, SLOTS], F32, name="gains")
        nc.sync.dma_start(out=gains[:], in_=gain.rearrange("(p t) -> p t", t=SLOTS))

        tab = [load_words(tab_words[0], "tab0")]
        load_table_scales(0)
        w1_raw = [load_rows(w1[:K_PASS, :], "w1_raw0")]
        load_table_scales(1)
        tab.append(load_words(tab_words[1], "tab1"))
        load_plane(nc.sync, w2_plane_raw, w2_scales)
        w1_raw.append(load_rows(w1[K_PASS:, :], "w1_raw1"))
        load_plane(nc.gpsimd, xs_plane, xs_scales)

        wx_raw, xs = {}, {}

        def load_wx(a, b):
            wx_raw[a, b] = load_rows(wx[K_PASS * a : K_PASS * (a + 1), K_PASS * b : K_PASS * (b + 1)], f"wx_raw{a}{b}")

        def load_xs(a, half):
            xs[a, half] = load_words(xs_words[a, :, half * HALF : (half + 1) * HALF, :], f"xs{a}{half}")

        load_wx(0, 0)
        load_xs(0, 0)
        w2_raw = kept([P, 2 * R], U8, "w2_raw")
        nc.sync.dma_start(out=w2_raw[:].bitcast(I32), in_=w2_words[0].bitcast(I32))
        load_wx(1, 0)
        load_xs(1, 0)
        load_wx(0, 1)
        load_xs(0, 1)
        load_xs(1, 1)
        load_wx(1, 1)
        wo_raw = []
        for b in range(2):
            raw = kept([P, SLOTS, N], F32, f"wo_raw{b}")
            rows = wo[K_PASS * b : K_PASS * (b + 1), :].rearrange("(g t i) n -> t g i n", t=SLOTS, i=RUN)
            for t in range(SLOTS):
                nc.sync.dma_start(out=raw[:, t, :], in_=rows[t])
            wo_raw.append(raw)
        floors = keep.tile([P, SCORE_TILES], F32, name="floors")
        with nc.allow_non_contiguous_dma(reason="one floor to a partition"):
            nc.sync.dma_start(out=floors[:], in_=floor_n.rearrange("(u p) -> p u", p=P))

        w1_codes, w1_plane = [], []

        def make_w1(a):
            values = ring.tile([P, SLOTS * H], BF16, name=f"w1_bf{a}", tag="rounded", align_bytes=64)
            dst = values[:].rearrange("p (t c j) -> p c j t", t=SLOTS, j=SLOTS)
            src = w1_raw[a][:].rearrange("p j (c t) -> p c j t", t=SLOTS)
            nc.scalar.copy(out=dst[:, :W1_SCALAR_SHARE], in_=src[:, :W1_SCALAR_SHARE])
            nc.vector.tensor_copy(out=dst[:, W1_SCALAR_SHARE:], in_=src[:, W1_SCALAR_SHARE:])
            w1_codes.append(kept([P, H], U32, f"w1_codes{a}"))
            w1_plane.append(kept([P, H], U8, f"w1_plane{a}"))
            for lo in range(0, H, H // 2):
                hi = lo + H // 2
                quantize(w1_codes[a][:, lo:hi], w1_plane[a][:, lo:hi], values[:, SLOTS * lo : SLOTS * hi])

        v_words = {}

        def gather_words(a):
            v_words[a] = kept([P, S], U32, f"v_words{a}")
            nc.vector.tensor_copy(v_words[a][:], tab[a][:].indirect(offsets[:]))

        minus_gain = keep.tile([P, SLOTS], F32, name="minus_gain")
        nc.vector.tensor_scalar(out=minus_gain[:], in0=gains[:], scalar1=-1.0, scalar2=None, op0=ALU.mult)
        gather_words(0)
        v_plane = kept([P, S], U8, "v_plane")
        nc.vector.tensor_copy(v_plane[:], tab_plane[:].indirect(offsets[:]))
        make_w1(0)
        w2_dealt = kept([P, 2 * R], U8, "w2_dealt")
        w2_plane = kept([P, R], U8, "w2_plane")
        nc.vector.tensor_copy(
            out=w2_plane[:].bitcast(I32).rearrange("p (b t g) -> p b t g", b=2, t=SLOTS),
            in_=w2_plane_raw[:].bitcast(I32).rearrange("p (b g t) -> p b t g", b=2, t=SLOTS),
        )
        gather_words(1)
        make_w1(1)

        lin = {}
        for a in range(2):
            for q in range(4):
                for pair in range(2):
                    if a == 0:
                        lin[q, pair] = bank(2 * q + pair, f"lin{q}{pair}")
                    for t in (2 * pair, 2 * pair + 1):
                        cols = slice(q * QUARTER, (q + 1) * QUARTER)
                        nc.tensor.matmul_mx(
                            out=lin[q, pair][:, (t % 2) * QUARTER : (t % 2 + 1) * QUARTER],
                            lhsT=w1_codes[a][:, t * P : (t + 1) * P].bitcast(FP8X4),
                            lhsT_scale=w1_plane[a][:, t * P : (t + 1) * P],
                            rhs=v_words[a][:, cols].bitcast(FP8X4),
                            rhs_scale=v_plane[4 * a :, cols],
                            start=(a == 0 and t % 2 == 0),
                            stop=(a == 1 and t % 2 == 1),
                        )

        bounded = []
        for q in range(4):
            bounded.append(ring.tile([P, SLOTS, QUARTER], F32, name=f"bounded{q}", tag="bounded", align_bytes=64))
            for t in range(SLOTS):
                nc.scalar.activation(
                    out=bounded[q][:, t, :],
                    in_=lin[q, t // 2][:, (t % 2) * QUARTER : (t % 2 + 1) * QUARTER],
                    func=ACT.Tanh,
                    bias=bias[:, t : t + 1],
                )

        h_codes, h_plane = [], []

        def make_h(q):
            values = ring.tile([P, SLOTS * QUARTER], BF16, name=f"h_bf{q}", tag="h_rounded", align_bytes=64)
            nc.vector.tensor_tensor(
                out=values[:].rearrange("p (c i t) -> p c t i", i=RUN, t=SLOTS),
                in0=bounded[q][:].rearrange("p t (c i) -> p c t i", i=RUN),
                in1=minus_gain[:].unsqueeze(1).unsqueeze(3).to_broadcast([P, QUARTER // RUN, SLOTS, RUN]),
                op=ALU.mult,
            )
            h_codes.append(kept([P, QUARTER], U32, f"h_codes{q}"))
            h_plane.append(kept([P, QUARTER], U8, f"h_plane{q}"))
            quantize(h_codes[q][:], h_plane[q][:], values[:])

        wx_codes, wx_plane = {}, {}

        def make_wx(a, b, scalar_slots):
            values = ring.tile([P, SLOTS * K_PASS], BF16, name=f"wx_bf{a}{b}", tag="rounded", align_bytes=64)
            dst = values[:].rearrange("p (t g i j) -> p g t j i", t=SLOTS, i=RUN, j=SLOTS)
            src = wx_raw[a, b][:].rearrange("p j (g t i) -> p g t j i", t=SLOTS, i=RUN)
            if scalar_slots:
                nc.scalar.copy(out=dst[:, :, :scalar_slots], in_=src[:, :, :scalar_slots])
            nc.vector.tensor_copy(out=dst[:, :, scalar_slots:], in_=src[:, :, scalar_slots:])
            wx_codes[a, b] = kept([P, K_PASS], U32, f"wx_codes{a}{b}")
            wx_plane[a, b] = kept([P, K_PASS], U8, f"wx_plane{a}{b}")
            quantize(wx_codes[a, b][:], wx_plane[a, b][:], values[:])

        wo_codes, wo_plane = [], []

        def make_wo(b):
            values = kept([P, SLOTS * N], BF16, f"wo_bf{b}")
            nc.vector.tensor_copy(
                out=values[:].rearrange("p (c i t) -> p c t i", i=RUN, t=SLOTS),
                in_=wo_raw[b][:].rearrange("p t (c i) -> p c t i", i=RUN),
            )
            wo_codes.append(kept([P, N], U32, f"wo_codes{b}"))
            wo_plane.append(kept([P, N], U8, f"wo_plane{b}"))
            for lo, hi in ((0, 2 * P), (2 * P, N)):
                quantize(wo_codes[b][:, lo:hi], wo_plane[b][:, lo:hi], values[:, SLOTS * lo : SLOTS * hi])

        z_rounded, z_values, z_tiles, z_codes, z_plane = {}, {}, {}, {}, {}

        def make_z(b, q, expect_at):
            key = (b, q // 2)
            if q % 2 == 0:
                room = "wx_raw11" if key == (0, 1) else None
                z_rounded[key] = kept([P, SLOTS * HALF], BF16, f"z_bf{b}{q // 2}", room)
            values = z_rounded[key][:, (q % 2) * SLOTS * QUARTER : (q % 2 + 1) * SLOTS * QUARTER]
            z_values[b, q] = values
            for e in range(2):
                acc = bank(2 * (q % 2) + (4 * b if q < 2 else 0) + e, f"diff{b}{q}{e}")
                cols = slice(q * QUARTER + e * P, q * QUARTER + (e + 1) * P)
                for step in range(3):
                    for t in range(SLOTS):
                        if step == expect_at:
                            lo = b * K_PASS + t * P
                            operands = dict(
                                lhsT=w2_dealt[:, 2 * lo : 2 * (lo + P)].bitcast(FP4X4),
                                lhsT_scale=w2_plane[:, lo : lo + P],
                                rhs=h_codes[q][:, e * P : (e + 1) * P].bitcast(FP8X4),
                                rhs_scale=h_plane[q][:, e * P : (e + 1) * P],
                            )
                        else:
                            a = step - (step > expect_at)
                            operands = dict(
                                lhsT=wx_codes[a, b][:, t * P : (t + 1) * P].bitcast(FP8X4),
                                lhsT_scale=wx_plane[a, b][:, t * P : (t + 1) * P],
                                rhs=xs[a, q // 2][:, cols.start % HALF : cols.start % HALF + P].bitcast(FP8X4),
                                rhs_scale=xs_plane[4 * a :, cols],
                            )
                        nc.tensor.matmul_mx(
                            out=acc[:, t * P : (t + 1) * P],
                            start=(step == 0 and t == 0),
                            stop=(step == 2 and t == SLOTS - 1),
                            **operands,
                        )
                nc.scalar.activation(
                    out=values[:, e * BANK : (e + 1) * BANK].rearrange("p (s t) -> p s t", t=SLOTS),
                    in_=acc[:].rearrange("p (t s) -> p s t", t=SLOTS),
                    func=ACT.Abs,
                )

        def quantize_z(b, q):
            piece = 4 * b + q
            room, first, count = ("z_early", 0, 2) if piece < 2 else ("wo_bf1", 2, 6)
            if room not in z_tiles:
                z_tiles[room] = kept([P, count * QUARTER], U32, f"z_codes{piece}", room)
            z_codes[b, q] = z_tiles[room][:, (piece - first) * QUARTER : (piece - first + 1) * QUARTER]
            z_plane[b, q] = kept([P, QUARTER], U8, f"z_plane{b}{q}")
            quantize(z_codes[b, q], z_plane[b, q][:], z_values[b, q])

        minus_floors = keep.tile([P, SCORE_TILES], F32, name="minus_floors")

        def make_scores(q):
            scores = ring.tile([P, SCORE_TILES, QUARTER], F32, name=f"scores{q}", tag="scores", align_bytes=64)
            last = q == 3
            if last:
                sums = [bank(2 + u, f"y{q}{u}")[:, :QUARTER] for u in range(SCORE_TILES)]
            else:
                banks = [bank((4 + 2 * q + n) % 8, f"y{q}{n}") for n in range(2)]
                sums = [banks[0][:, :QUARTER], banks[1][:, :QUARTER], banks[1][:, QUARTER:]]
            for u in range(SCORE_TILES):
                for b in range(2):
                    nc.tensor.matmul_mx(
                        out=sums[u],
                        lhsT=wo_codes[b][:, u * P : (u + 1) * P].bitcast(FP8X4),
                        lhsT_scale=wo_plane[b][:, u * P : (u + 1) * P],
                        rhs=z_codes[b, q].bitcast(FP8X4),
                        rhs_scale=z_plane[b, q][:],
                        start=(b == 0),
                        stop=(b == 1),
                    )
            for u in range(SCORE_TILES):
                floor = floors[:, u : u + 1]
                if u == 0:
                    above = ring.tile([P, QUARTER], F32, name=f"above{q}", tag="above")
                    nc.scalar.activation(out=above[:], in_=sums[u], func=ACT.Relu, bias=minus_floors[:, u : u + 1])
                    nc.scalar.activation(out=scores[:, u, :], in_=above[:], func=ACT.Identity, bias=floor)
                else:
                    nc.vector.tensor_scalar(out=scores[:, u, :], in0=sums[u], scalar1=floor, scalar2=None, op0=ALU.max)
                if last:
                    nc.sync.dma_start(out=out[u * P : (u + 1) * P, q * QUARTER :], in_=scores[:, u, :])
            if not last:
                nc.sync.dma_start(
                    out=out[:, q * QUARTER : (q + 1) * QUARTER].rearrange("(u p) s -> p u s", p=P), in_=scores[:]
                )

        make_wx(0, 0, scalar_slots=0)
        make_h(0)
        nc.vector.tensor_copy(
            out=w2_dealt[:].bitcast(I32).rearrange("p (b t g w) -> p b t g w", b=2, t=SLOTS, w=2),
            in_=w2_raw[:].bitcast(I32).rearrange("p (b g t w) -> p b t g w", b=2, t=SLOTS, w=2),
        )
        make_wx(1, 0, scalar_slots=2)
        make_h(1)
        make_z(0, 0, expect_at=1)
        make_z(0, 1, expect_at=1)
        make_wx(0, 1, scalar_slots=2)
        make_h(2)
        make_wx(1, 1, scalar_slots=2)
        make_z(0, 2, expect_at=2)
        make_h(3)
        make_z(0, 3, expect_at=2)
        make_wo(0)
        make_wo(1)
        nc.vector.tensor_scalar(out=minus_floors[:], in0=floors[:], scalar1=-1.0, scalar2=None, op0=ALU.mult)
        make_z(1, 0, expect_at=0)
        make_z(1, 1, expect_at=0)
        make_z(1, 2, expect_at=1)
        for q in range(4):
            if q == 1:
                make_z(1, 3, expect_at=1)
            quantize_z(0, q)
            quantize_z(1, q)
            make_scores(q)
